import numpy as np
import ml_dtypes


def mxq(x, axis, fmt="e4m3"):
    dtype, down = {"e4m3": (ml_dtypes.float8_e4m3fn, 7), "e5m2": (ml_dtypes.float8_e5m2, 14)}[fmt]
    v = np.moveaxis(np.asarray(x, np.float32).astype(ml_dtypes.bfloat16).astype(np.float64), axis, -1)
    blocks = v.reshape(v.shape[:-1] + (-1, 32))
    amax = np.abs(blocks).max(-1, keepdims=True)
    byte = np.maximum(np.where(amax > 0, np.frexp(amax)[1] - 1 + 127, 0) - down, 1)
    scale = np.exp2(byte - 127.0)
    codes = (blocks / scale).astype(np.float32).astype(dtype).astype(np.float64)
    return np.moveaxis((codes * scale).reshape(v.shape), -1, axis)


WIDE = False


def mx_kscale(k):
    if not WIDE:
        return np.ones(k)
    levels = np.array([10, -10, 5, -5, 0])
    if k % 512:
        return np.exp2(np.random.permutation(np.resize(levels, k // 32))).repeat(32)
    a = np.empty((k // 512, 16))
    for p in range(k // 512):
        a[p, :8] = np.random.permutation(np.resize(levels, 8))
        for g in range(8):
            far = levels[np.abs(levels - a[p, g]) >= 10]
            a[p, g + 8] = far[np.random.randint(len(far))]
    return np.exp2(a.ravel()).repeat(32)


def f64(x):
    return np.asarray(x).astype(np.float64)


def striped(idx):
    return np.tile(idx.reshape(-1, 16).T, (8, 1)).astype(np.uint16)


def unstriped(offs):
    return offs[:16].T.reshape(-1).astype(np.int64)


E2M1 = np.array([0.0, 0.5, 1.0, 1.5, 2.0, 3.0, 4.0, 6.0, -0.0, -0.5, -1.0, -1.5, -2.0, -3.0, -4.0, -6.0])


def pack_weight(w, fmt):
    k, n = w.shape
    w = f64(np.asarray(w, np.float32).astype(ml_dtypes.bfloat16)).reshape(k // 32, 32, n)
    amax = np.abs(w).max(1)
    if fmt == "e4m3":
        byte = np.frexp(amax)[1] - 1 + 127 - 7
    else:
        mant, ex = np.frexp(amax / 6.0)
        byte = np.where(mant > 0.5, ex, ex - 1) + 127
    byte = np.clip(np.where(amax > 0, byte, 1), 1, 254)
    scaled = (w * np.exp2(127.0 - byte)[:, None, :]).reshape(k, n).astype(np.float32)
    by_word = np.ascontiguousarray(scaled.reshape(k // 512, 128, 4, n).transpose(0, 1, 3, 2))
    if fmt == "e4m3":
        words = by_word.astype(ml_dtypes.float8_e4m3fn).view(np.uint8)
    else:
        c = by_word.astype(ml_dtypes.float4_e2m1fn).view(np.uint8) & 0xF
        words = (c[..., 0::2] | (c[..., 1::2] << 4)).reshape(k // 512, 128, 2 * n)
    return np.ascontiguousarray(words), np.ascontiguousarray(byte.astype(np.uint8).reshape(k // 512, 16, n))


def unpack_weight(words, scales, fmt):
    g, _, n = scales.shape
    words = np.ascontiguousarray(words).reshape(g, 128, n, -1)
    if fmt == "e4m3":
        vals = words.view(ml_dtypes.float8_e4m3fn).astype(np.float64)
    else:
        nib = np.empty((g, 128, n, 4), np.uint8)
        nib[..., 0::2] = words & 0xF
        nib[..., 1::2] = words >> 4
        vals = E2M1[nib]
    vals = vals * np.repeat(np.exp2(scales.astype(np.float64) - 127.0), 8, axis=1)[..., None]
    return vals.transpose(0, 1, 3, 2).reshape(g * 512, n)


def gelu(v):
    return 0.5 * v * (1.0 + np.tanh(np.sqrt(2.0 / np.pi) * (v + 0.044715 * v**3)))


K, T, S, P, H, N = 1536, 4096, 1024, 512, 1024, 512


def setup_inputs():
    n = np.random.standard_normal
    s = mx_kscale(K)[:, None]
    u = mx_kscale(H)[:, None]
    tab_words, tab_scales = pack_weight(n((K, T)) * s, "e4m3")
    w4_words, w4_scales = pack_weight(n((H, N)) / np.sqrt(H) / u, "e2m1")
    perm = np.random.permutation(S)
    return {
        "tab_words": tab_words, "tab_scales": tab_scales,
        "offs": striped(np.random.permutation(T)[:S]),
        "pos1": striped(perm[:P]),
        "pos2": striped(perm[P:]),
        "w1": (0.95 * n((K, H)) / np.sqrt(K) / s).astype(np.float32),
        "thr": n(H).astype(np.float32),
        "weft": (2.5 * n((H, P))).astype(np.float32),
        "skip": np.random.uniform(0.2, 0.8, H).astype(np.float32),
        "wgs": np.exp(0.3 * n((128, P))).astype(np.float32),
        "gain": (np.random.uniform(0.6, 1.4, H) * u[:, 0]).astype(np.float32),
        "w4_words": w4_words, "w4_scales": w4_scales,
    }


def reference(tab_words, tab_scales, offs, pos1, pos2, w1, thr, weft, skip, wgs, gain, w4_words, w4_scales):
    v = unpack_weight(tab_words, tab_scales, "e4m3")[:, unstriped(offs)]
    w1q = mxq(f64(w1), 0, "e4m3")
    h = w1q.T @ v
    look = 1.0 / (1.0 + np.exp(-(h[:, unstriped(pos1)] + f64(thr)[:, None])))
    a = f64(weft) * look
    page = f64(skip)[:, None] * h
    page[:, unstriped(pos2)] = np.tile(f64(wgs), (H // 128, 1)) * a
    z = mxq(f64(gain)[:, None] * (page + h), 0, "e4m3")
    w4 = unpack_weight(w4_words, w4_scales, "e2m1")
    y = w4.T @ z
    return y

@@ -1,0 +1,329 @@
+from contextlib import ExitStack
+
+import concourse.mybir as mybir
+from concourse.masks import make_identity
+
+K, T, S, NP, H, N = 1536, 4096, 1024, 512, 1024, 512
+FLOPS = 2 * K * H * S + 2 * H * N * S
+
+F32 = mybir.dt.float32
+BF16 = mybir.dt.bfloat16
+I32 = mybir.dt.int32
+U32 = mybir.dt.uint32
+U16 = mybir.dt.uint16
+U8 = mybir.dt.uint8
+FP8X4 = mybir.dt.float8_e4m3fn_x4
+FP4X4 = mybir.dt.float4_e2m1fn_x4
+MULT = mybir.AluOpType.mult
+ACT = mybir.ActivationFunctionType
+
+P = 128
+PACK = 4
+K_PASS = P * PACK
+BANK = 512
+KP = K // K_PASS
+HP = H // K_PASS
+SLICES = H // P
+HALVES = S // BANK
+QUARTER = 2 * P
+W1_LOADS = [(0, 1), (1, 1), (2, 2), (4, 4)]
+
+
+def tile_list_weft_fault_repair_kernel(tc, tab_words, tab_scales, offs, pos1, pos2, w1, thr, weft, skip, wgs, gain, w4_words, w4_scales, out):
+    nc = tc.nc
+    with ExitStack() as ctx:
+        lists = ctx.enter_context(tc.tile_pool(name="lists", bufs=1))
+        keep = ctx.enter_context(tc.tile_pool(name="keep", bufs=1))
+        ring = ctx.enter_context(tc.tile_pool(name="ring", bufs=1))
+        psum = ctx.enter_context(tc.psum_pool(name="psum", bufs=1))
+
+        offs_t = lists.tile([P, S // 16], U16, name="offs_t")
+        pos1_t = lists.tile([P, NP // 16], U16, name="pos1_t")
+        pos2_t = lists.tile([P, NP // 16], U16, name="pos2_t")
+
+        tab_s = keep.tile([P, T], U8, name="tab_s", align_bytes=64)
+        rows = keep.tile([P, P], F32, name="rows")
+        w4_s = keep.tile([P, HP, N], U8, name="w4_s", align_bytes=64)
+        w4_w = keep.tile([P, HP, 2 * N], U8, name="w4_w", align_bytes=64)
+        ident = keep.tile([P, P], F32, name="ident")
+        make_identity(nc, ident[:])
+        nc.vector.memset(rows[:], 0.0)
+        nc.vector.memset(tab_s[:].bitcast(I32), 0)
+        nc.vector.memset(w4_s[:].rearrange("p a n -> p (a n)").bitcast(I32), 0)
+
+        nc.sync.dma_start(offs_t[:], offs)
+        tab_w = []
+
+        def load_table(a):
+            t = ring.tile([P, T], I32, name="tab_w%d" % a, tag="big", bufs=3, align_bytes=64)
+            nc.sync.dma_start(t[:], tab_words[a].rearrange("p t i -> p (t i)").bitcast(I32))
+            tab_w.append(t)
+
+        load_table(0)
+        for i, vec in enumerate((thr, skip, gain)):
+            nc.sync.dma_start(rows[SLICES * i : SLICES * (i + 1), :], vec.rearrange("(s p) -> s p", p=P))
+        nc.sync.dma_start(pos1_t[:], pos1)
+        nc.sync.dma_start(pos2_t[:], pos2)
+        load_table(1)
+        for q in range(4):
+            nc.gpsimd.dma_start(tab_s[32 * q : 32 * q + 4 * KP, :].bitcast(I32), tab_scales[:, 4 * q : 4 * q + 4, :].bitcast(I32))
+
+        w1_raw = {}
+        weft_t = {}
+        wgs_t = keep.tile([P, NP], F32, name="wgs_t")
+
+        def load_w1(first, count, passes=range(KP)):
+            for a in passes:
+                if count == 4:
+                    t = ring.tile([P, PACK, count * P], F32, name="w1_%d_%d" % (first, a), tag="big", bufs=3, align_bytes=64)
+                else:
+                    t = keep.tile([P, PACK, count * P], F32, name="w1_%d_%d" % (first, a))
+                nc.sync.dma_start(t[:], w1[a * K_PASS : (a + 1) * K_PASS, first * P : (first + count) * P].rearrange("(p j) c -> p j c", j=PACK))
+                for s in range(first, first + count):
+                    w1_raw[(s, a)] = t[:, :, (s - first) * P : (s - first + 1) * P]
+
+        def load_weft(first, count):
+            t = keep.tile([P, count, NP], F32, name="weft_%d" % first)
+            nc.sync.dma_start(t[:], weft[first * P : (first + count) * P, :].rearrange("(s p) m -> p s m", p=P))
+            for s in range(first, first + count):
+                weft_t[s] = t[:, s - first, :]
+
+        load_w1(0, 1, range(KP - 1))
+        load_table(KP - 1)
+        load_w1(0, 1, [KP - 1])
+        load_w1(1, 1)
+        nc.sync.dma_start(wgs_t[:], wgs)
+        load_weft(0, 1)
+
+        v_s = keep.tile([P, S], U8, name="v_s", align_bytes=64)
+        v_w = {}
+
+        def gather_whole(a):
+            t = keep.tile([P, S], U32, name="v_w%d" % a, align_bytes=64)
+            nc.vector.tensor_copy(t[:], tab_w[a][:].bitcast(U32).indirect(offs_t[:]))
+            for f in range(HALVES):
+                v_w[(a, f)] = t[:, f * BANK : (f + 1) * BANK]
+
+        def gather_half(a, f):
+            t = ring.tile([P, BANK], U32, name="v_w%d_%d" % (a, f), tag="late%d" % f, align_bytes=64)
+            c = BANK // 16
+            nc.vector.tensor_copy(t[:], tab_w[a][:].bitcast(U32).indirect(offs_t[:, f * c : (f + 1) * c]))
+            v_w[(a, f)] = t[:]
+
+        gather_whole(0)
+        nc.vector.tensor_copy(v_s[:], tab_s[:].indirect(offs_t[:]))
+        gather_whole(1)
+        gather_half(KP - 1, 0)
+        load_w1(2, 1)
+        load_weft(1, 1)
+        load_w1(3, 1)
+        load_weft(2, 2)
+        load_w1(4, 4)
+        load_weft(4, 4)
+        nc.sync.dma_start(w4_w[:].bitcast(I32), w4_words.rearrange("a p n -> p a n").bitcast(I32))
+
+        for q in range(4):
+            nc.sync.dma_start(
+                w4_s[32 * q : 32 * q + 4, :, :].bitcast(I32),
+                w4_scales[:, 4 * q : 4 * q + 4, :].rearrange("a r n -> r a n").bitcast(I32),
+            )
+
+        cols = keep.tile([P, 3 * SLICES], F32, name="cols")
+        bank = psum.tile([P, BANK], F32, name="bank_c", tag="o0")
+        nc.tensor.transpose(bank[:, 0:P], rows[:], ident[:])
+        nc.scalar.copy(cols[:], bank[:, 0 : 3 * SLICES])
+        gain_bc = keep.tile([P, SLICES, P], F32, name="gain_bc")
+        for g in range(HP):
+            bank = psum.tile([P, PACK, P], F32, name="bank_g%d" % g, tag="w%d" % g)
+            for i in range(PACK):
+                c = 2 * SLICES + PACK * g + i
+                nc.tensor.transpose(bank[:, i, :], cols[:, c : c + 1].to_broadcast([P, P]), ident[:])
+            nc.scalar.copy(
+                gain_bc[:, PACK * g : PACK * (g + 1), :].rearrange("j i (u q e) -> j i u q e", u=2, e=2),
+                bank[:].rearrange("j i (q u e) -> j i u q e", u=2, e=2),
+            )
+
+        w1_q = {}
+        w1_s = [keep.tile([P, KP * P], U8, name="w1_s%d" % s, align_bytes=64) for s in range(SLICES)]
+        w1_b = {}
+        h_banks = {}
+        h_t = {}
+        look_t = {}
+        page_t = {}
+        ww_t = {}
+        sum_banks = {}
+        z_t = {(b, f): keep.tile([P, PACK, K_PASS], BF16, name="z_t%d_%d" % (b, f), align_bytes=64) for b in range(HP) for f in range(HALVES)}
+        z_q = [keep.tile([P, S], U32, name="z_q%d" % b, align_bytes=64) for b in range(HP)]
+        z_s = [keep.tile([P, S], U8, name="z_s%d" % b, align_bytes=64) for b in range(HP)]
+
+        def cast_w1(s):
+            if s == 0:
+                parts = [ring.tile([P, P * PACK], BF16, name="w1_b0_%d" % a, tag="late1" if a == KP - 1 else "w1_b0_%d" % a, align_bytes=64)[:] for a in range(KP)]
+                w1_b[s] = parts
+            else:
+                t = ring.tile([P, KP, P * PACK], BF16, name="w1_b%d" % s, tag="w1_b", bufs=3, align_bytes=64)
+                parts = [t[:, a, :] for a in range(KP)]
+                w1_b[s] = t
+            for a in range(KP):
+                dst = parts[a].rearrange("p (c i j) -> p c j i", i=4, j=PACK)
+                src = w1_raw[(s, a)].rearrange("p j (c i) -> p c j i", i=4)
+                if (s, a) == (1, KP - 1):
+                    nc.vector.tensor_copy(dst, src)
+                else:
+                    nc.scalar.copy(dst, src)
+
+        def quant_w1(s):
+            if s < 2:
+                w1_q[s] = keep.tile([P, KP * P], U32, name="w1_q%d" % s, align_bytes=64)
+            else:
+                w1_q[s] = ring.tile([P, KP * P], U32, name="w1_q%d" % s, tag="look%d" % (s % 2), align_bytes=64)
+            if s == 0:
+                for a in range(KP):
+                    c = slice(a * P, (a + 1) * P)
+                    nc.vector.quantize_mx(out=w1_q[s][:, c].bitcast(FP8X4), scales=w1_s[s][:, c], in_=w1_b[s][a])
+            else:
+                nc.vector.quantize_mx(out=w1_q[s][:].bitcast(FP8X4), scales=w1_s[s][:], in_=w1_b[s][:].rearrange("p a c -> p (a c)"))
+
+        def first_product(s):
+            banks = [psum.tile([P, BANK], F32, name="h_b%d_%d" % (s, f), tag="h%d" % f) for f in range(HALVES)]
+            for a in range(KP):
+                c = slice(a * P, (a + 1) * P)
+                for f in range(HALVES):
+                    j = slice(f * BANK, (f + 1) * BANK)
+                    nc.tensor.matmul_mx(
+                        out=banks[f][:], lhsT=w1_q[s][:, c].bitcast(FP8X4), lhsT_scale=w1_s[s][:, c],
+                        rhs=v_w[(a, f)].bitcast(FP8X4), rhs_scale=v_s[4 * a :, j], start=(a == 0), stop=(a == KP - 1),
+                    )
+            h_banks[s] = banks
+
+        def copy_h(s):
+            t = ring.tile([P, S], F32, name="h%d" % s, tag="h", bufs=3)
+            for f in range(HALVES):
+                j = slice(f * BANK, (f + 1) * BANK)
+                if (s, f) == (0, 0):
+                    nc.vector.tensor_copy(t[:, j], h_banks[s][f][:])
+                else:
+                    nc.scalar.copy(t[:, j], h_banks[s][f][:])
+            h_t[s] = t
+
+        def look(s):
+            t = ring.tile([P, NP], F32, name="look%d" % s, tag="look%d" % (s % 2), align_bytes=64)
+            nc.scalar.activation(out=t[:], in_=h_t[s][:].indirect(pos1_t[:]), func=ACT.Sigmoid, bias=cols[:, s : s + 1])
+            look_t[s] = t
+
+        def fill_page(s):
+            t = ring.tile([P, S], F32, name="page%d" % s, tag="page", bufs=3)
+            col = cols[:, SLICES + s : SLICES + s + 1]
+            if s == 0:
+                nc.vector.tensor_scalar(out=t[:], in0=h_t[s][:], scalar1=col, scalar2=None, op0=MULT)
+            else:
+                nc.scalar.activation(out=t[:], in_=h_t[s][:], func=ACT.Copy, scale=col)
+            page_t[s] = t
+
+        def weigh(s):
+            t = ring.tile([P, NP], F32, name="ww%d" % s, tag="ww", bufs=1)
+            nc.vector.tensor_tensor(t[:], weft_t[s], wgs_t[:], MULT)
+            ww_t[s] = t
+
+        def scatter(s):
+            nc.vector.tensor_tensor(page_t[s][:].indirect(pos2_t[:]), look_t[s][:], ww_t[s][:], MULT)
+
+        def turn(s, src, first):
+            if first:
+                sum_banks[s] = [psum.tile([P, PACK, P], F32, name="t_b%d_%d" % (s, f), tag=("o%d" if s == SLICES - 1 else "t%d") % f) for f in range(HALVES)]
+            for f in range(HALVES):
+                for c in range(PACK):
+                    jc = PACK * f + c
+                    nc.tensor.matmul(
+                        sum_banks[s][f][:, c, :], src[:, jc * P : (jc + 1) * P], ident[:], is_transpose=True,
+                        start=(first and c == 0), stop=(not first and c == PACK - 1),
+                    )
+
+        def round_z(s):
+            b, i = divmod(s, PACK)
+            for f in range(HALVES):
+                nc.vector.tensor_tensor(
+                    z_t[(b, f)][:].rearrange("j c (u i q e) -> j i u c q e", u=2, i=PACK, e=2)[:, i],
+                    sum_banks[s][f][:].rearrange("j c (q u e) -> j u c q e", u=2, e=2),
+                    gain_bc[:, s : s + 1, :].to_broadcast([P, PACK, P]).rearrange("j c (u q e) -> j u c q e", u=2, e=2), MULT,
+                )
+
+        def turn_back(b, q, tag):
+            zi = ring.tile([P, QUARTER * PACK], BF16, name="zi%d_%d" % (b, q), tag="zi", bufs=4, align_bytes=64)
+            bank = psum.tile([P, 2, 2, P], F32, name="w_b%d_%d" % (b, q), tag=tag)
+            for c in range(2):
+                words = z_t[(b, q // 2)][:, 2 * (q % 2) + c, :].bitcast(F32)
+                for u in range(2):
+                    nc.tensor.transpose(bank[:, c, u, :], words[:, u * P : (u + 1) * P], ident[:])
+            nc.scalar.copy(zi[:].bitcast(F32).rearrange("p (c j u) -> p c j u", c=2, u=2), bank[:].rearrange("p c u j -> p c j u"))
+            j = slice(q * QUARTER, (q + 1) * QUARTER)
+            nc.vector.quantize_mx(out=z_q[b][:, j].bitcast(FP8X4), scales=z_s[b][:, j], in_=zi[:])
+
+        out_banks = {}
+
+        def second_product(b, q, g, tag=None):
+            if b == 0:
+                out_banks[(q, g)] = psum.tile([P, 2, QUARTER], F32, name="o_b%d_%d" % (q, g), tag=tag)
+            j = slice(q * QUARTER, (q + 1) * QUARTER)
+            for m in range(2):
+                n = 2 * g + m
+                nc.tensor.matmul_mx(
+                    out=out_banks[(q, g)][:, m, :], lhsT=w4_w[:, b, 2 * P * n : 2 * P * (n + 1)].bitcast(FP4X4), lhsT_scale=w4_s[:, b, P * n : P * (n + 1)],
+                    rhs=z_q[b][:, j].bitcast(FP8X4), rhs_scale=z_s[b][:, j], start=(b == 0 and m == 0), stop=(b == HP - 1 and m == 1),
+                )
+
+        def store(q, g):
+            t = ring.tile([P, 2, QUARTER], F32, name="res%d_%d" % (q, g), tag="res", bufs=8)
+            if g == 0:
+                nc.scalar.copy(t[:], out_banks[(q, g)][:])
+            else:
+                nc.vector.tensor_copy(t[:], out_banks[(q, g)][:])
+            rows_out = out[2 * g * P : 2 * (g + 1) * P, q * QUARTER : (q + 1) * QUARTER]
+            nc.sync.dma_start(rows_out.rearrange("(m p) j -> p m j", p=P), t[:])
+
+        cast_w1(0)
+        quant_w1(0)
+        gather_half(KP - 1, 1)
+        first_product(0)
+        copy_h(0)
+        look(0)
+        fill_page(0)
+        weigh(0)
+        cast_w1(1)
+        quant_w1(1)
+        first_product(1)
+        cast_w1(2)
+        turn(0, h_t[0], True)
+        for s in range(SLICES):
+            scatter(s)
+            turn(s, page_t[s], False)
+            if s + 1 < SLICES:
+                copy_h(s + 1)
+                look(s + 1)
+                fill_page(s + 1)
+                weigh(s + 1)
+            if s == 0:
+                cast_w1(3)
+            if s + 2 < SLICES:
+                quant_w1(s + 2)
+                first_product(s + 2)
+            if s + 4 < SLICES:
+                cast_w1(s + 4)
+            round_z(s)
+            if s + 1 < SLICES:
+                turn(s + 1, h_t[s + 1], True)
+            if s in (PACK, PACK + 1):
+                for g in range(2):
+                    turn_back(0, 2 * (s - PACK) + g, "w%d" % g)
+            if s == SLICES - 2:
+                for g in range(2):
+                    second_product(0, 0, g, "t%d" % g)
+        for q, tag in enumerate(("h0", "h1", "w0", "w1")):
+            turn_back(1, q, tag)
+        for q, tags in enumerate((None, "h%d", "o%d", "w%d")):
+            for g in range(2):
+                if tags is not None:
+                    second_product(0, q, g, tags % g)
+            for g in range(2):
+                second_product(1, q, g)
+                store(q, g)

@@ -26,7 +26,8 @@ HP = H // K_PASS
 SLICES = H // P
 HALVES = S // BANK
 QUARTER = 2 * P
-W1_LOADS = [(0, 1), (1, 1), (2, 2), (4, 4)]
+V_CASTS = [(1, 2), (2, 2), (3, 1), (3, 2)]
+LAST = SLICES - 1
 
 
 def tile_list_weft_fault_repair_kernel(tc, tab_words, tab_scales, offs, pos1, pos2, w1, thr, weft, skip, wgs, gain, w4_words, w4_scales, out):
@@ -41,41 +42,39 @@ def tile_list_weft_fault_repair_kernel(tc, tab_words, tab_scales, offs, pos1, po
         pos1_t = lists.tile([P, NP // 16], U16, name="pos1_t")
         pos2_t = lists.tile([P, NP // 16], U16, name="pos2_t")
 
-        tab_s = keep.tile([P, T], U8, name="tab_s", align_bytes=64)
+        tab_s = ring.tile([P, T], U8, name="tab_s", tag="v_w1", align_bytes=64)
         rows = keep.tile([P, P], F32, name="rows")
         w4_s = keep.tile([P, HP, N], U8, name="w4_s", align_bytes=64)
         w4_w = keep.tile([P, HP, 2 * N], U8, name="w4_w", align_bytes=64)
         ident = keep.tile([P, P], F32, name="ident")
         make_identity(nc, ident[:])
-        nc.vector.memset(rows[:], 0.0)
         nc.vector.memset(tab_s[:].bitcast(I32), 0)
+        nc.vector.memset(rows[:], 0.0)
         nc.vector.memset(w4_s[:].rearrange("p a n -> p (a n)").bitcast(I32), 0)
 
         nc.sync.dma_start(offs_t[:], offs)
         tab_w = []
 
         def load_table(a):
-            t = ring.tile([P, T], I32, name="tab_w%d" % a, tag="big", bufs=3, align_bytes=64)
+            t = ring.tile([P, T], I32, name="tab_w%d" % a, tag="tab%d" % a, align_bytes=64)
             nc.sync.dma_start(t[:], tab_words[a].rearrange("p t i -> p (t i)").bitcast(I32))
             tab_w.append(t)
 
         load_table(0)
+        for q in range(4):
+            nc.sync.dma_start(tab_s[32 * q : 32 * q + 4 * KP, :].bitcast(I32), tab_scales[:, 4 * q : 4 * q + 4, :].bitcast(I32))
+        load_table(1)
         for i, vec in enumerate((thr, skip, gain)):
             nc.sync.dma_start(rows[SLICES * i : SLICES * (i + 1), :], vec.rearrange("(s p) -> s p", p=P))
-        nc.sync.dma_start(pos1_t[:], pos1)
-        nc.sync.dma_start(pos2_t[:], pos2)
-        load_table(1)
-        for q in range(4):
-            nc.gpsimd.dma_start(tab_s[32 * q : 32 * q + 4 * KP, :].bitcast(I32), tab_scales[:, 4 * q : 4 * q + 4, :].bitcast(I32))
 
         w1_raw = {}
         weft_t = {}
         wgs_t = keep.tile([P, NP], F32, name="wgs_t")
 
-        def load_w1(first, count, passes=range(KP)):
-            for a in passes:
-                if count == 4:
-                    t = ring.tile([P, PACK, count * P], F32, name="w1_%d_%d" % (first, a), tag="big", bufs=3, align_bytes=64)
+        def load_w1(first, count):
+            for a in range(KP):
+                if first == 6:
+                    t = late[:, a]
                 else:
                     t = keep.tile([P, PACK, count * P], F32, name="w1_%d_%d" % (first, a))
                 nc.sync.dma_start(t[:], w1[a * K_PASS : (a + 1) * K_PASS, first * P : (first + count) * P].rearrange("(p j) c -> p j c", j=PACK))
@@ -88,9 +87,10 @@ def tile_list_weft_fault_repair_kernel(tc, tab_words, tab_scales, offs, pos1, po
             for s in range(first, first + count):
                 weft_t[s] = t[:, s - first, :]
 
-        load_w1(0, 1, range(KP - 1))
         load_table(KP - 1)
-        load_w1(0, 1, [KP - 1])
+        load_w1(0, 1)
+        nc.sync.dma_start(pos1_t[:], pos1)
+        nc.sync.dma_start(pos2_t[:], pos2)
         load_w1(1, 1)
         nc.sync.dma_start(wgs_t[:], wgs)
         load_weft(0, 1)
@@ -98,27 +98,19 @@ def tile_list_weft_fault_repair_kernel(tc, tab_words, tab_scales, offs, pos1, po
         v_s = keep.tile([P, S], U8, name="v_s", align_bytes=64)
         v_w = {}
 
-        def gather_whole(a):
-            t = keep.tile([P, S], U32, name="v_w%d" % a, align_bytes=64)
+        for a in range(KP):
+            t = ring.tile([P, S], U32, name="v_w%d" % a, tag=("v_w0", "v_w1", "tab1")[a], align_bytes=64)
             nc.vector.tensor_copy(t[:], tab_w[a][:].bitcast(U32).indirect(offs_t[:]))
-            for f in range(HALVES):
-                v_w[(a, f)] = t[:, f * BANK : (f + 1) * BANK]
+            v_w[a] = t
+            if a == 0:
+                nc.vector.tensor_copy(v_s[:], tab_s[:].indirect(offs_t[:]))
 
-        def gather_half(a, f):
-            t = ring.tile([P, BANK], U32, name="v_w%d_%d" % (a, f), tag="late%d" % f, align_bytes=64)
-            c = BANK // 16
-            nc.vector.tensor_copy(t[:], tab_w[a][:].bitcast(U32).indirect(offs_t[:, f * c : (f + 1) * c]))
-            v_w[(a, f)] = t[:]
-
-        gather_whole(0)
-        nc.vector.tensor_copy(v_s[:], tab_s[:].indirect(offs_t[:]))
-        gather_whole(1)
-        gather_half(KP - 1, 0)
-        load_w1(2, 1)
+        load_w1(2, 2)
         load_weft(1, 1)
-        load_w1(3, 1)
+        load_w1(4, 2)
         load_weft(2, 2)
-        load_w1(4, 4)
+        late = ring.tile([P, KP, PACK, 2 * P], F32, name="w1_late", tag="tab0", align_bytes=64)
+        load_w1(6, 2)
         load_weft(4, 4)
         nc.sync.dma_start(w4_w[:].bitcast(I32), w4_words.rearrange("a p n -> p a n").bitcast(I32))
 
@@ -129,12 +121,12 @@ def tile_list_weft_fault_repair_kernel(tc, tab_words, tab_scales, offs, pos1, po
             )
 
         cols = keep.tile([P, 3 * SLICES], F32, name="cols")
-        bank = psum.tile([P, BANK], F32, name="bank_c", tag="o0")
+        bank = psum.tile([P, BANK], F32, name="bank_c", tag="w1")
         nc.tensor.transpose(bank[:, 0:P], rows[:], ident[:])
         nc.scalar.copy(cols[:], bank[:, 0 : 3 * SLICES])
         gain_bc = keep.tile([P, SLICES, P], F32, name="gain_bc")
         for g in range(HP):
-            bank = psum.tile([P, PACK, P], F32, name="bank_g%d" % g, tag="w%d" % g)
+            bank = psum.tile([P, PACK, P], F32, name="bank_g%d" % g, tag="o%d" % g)
             for i in range(PACK):
                 c = 2 * SLICES + PACK * g + i
                 nc.tensor.transpose(bank[:, i, :], cols[:, c : c + 1].to_broadcast([P, P]), ident[:])
@@ -157,57 +149,49 @@ def tile_list_weft_fault_repair_kernel(tc, tab_words, tab_scales, offs, pos1, po
         z_s = [keep.tile([P, S], U8, name="z_s%d" % b, align_bytes=64) for b in range(HP)]
 
         def cast_w1(s):
-            if s == 0:
-                parts = [ring.tile([P, P * PACK], BF16, name="w1_b0_%d" % a, tag="late1" if a == KP - 1 else "w1_b0_%d" % a, align_bytes=64)[:] for a in range(KP)]
-                w1_b[s] = parts
-            else:
-                t = ring.tile([P, KP, P * PACK], BF16, name="w1_b%d" % s, tag="w1_b", bufs=3, align_bytes=64)
-                parts = [t[:, a, :] for a in range(KP)]
-                w1_b[s] = t
+            t = ring.tile([P, KP, P * PACK], BF16, name="w1_b%d" % s, tag="w1_b", bufs=3, align_bytes=64)
             for a in range(KP):
-                dst = parts[a].rearrange("p (c i j) -> p c j i", i=4, j=PACK)
+                dst = t[:, a, :].rearrange("p (c i j) -> p c j i", i=4, j=PACK)
                 src = w1_raw[(s, a)].rearrange("p j (c i) -> p c j i", i=4)
-                if (s, a) == (1, KP - 1):
+                if (s, a) in V_CASTS:
                     nc.vector.tensor_copy(dst, src)
                 else:
                     nc.scalar.copy(dst, src)
+            w1_b[s] = t
 
         def quant_w1(s):
-            if s < 2:
-                w1_q[s] = keep.tile([P, KP * P], U32, name="w1_q%d" % s, align_bytes=64)
-            else:
-                w1_q[s] = ring.tile([P, KP * P], U32, name="w1_q%d" % s, tag="look%d" % (s % 2), align_bytes=64)
+            w1_q[s] = ring.tile([P, KP * P], U32, name="w1_q%d" % s, tag="tab2" if s == 0 else "w1_q%d" % s, align_bytes=64)
             if s == 0:
                 for a in range(KP):
                     c = slice(a * P, (a + 1) * P)
-                    nc.vector.quantize_mx(out=w1_q[s][:, c].bitcast(FP8X4), scales=w1_s[s][:, c], in_=w1_b[s][a])
+                    nc.vector.quantize_mx(out=w1_q[s][:, c].bitcast(FP8X4), scales=w1_s[s][:, c], in_=w1_b[s][:, a, :])
             else:
                 nc.vector.quantize_mx(out=w1_q[s][:].bitcast(FP8X4), scales=w1_s[s][:], in_=w1_b[s][:].rearrange("p a c -> p (a c)"))
 
         def first_product(s):
-            banks = [psum.tile([P, BANK], F32, name="h_b%d_%d" % (s, f), tag="h%d" % f) for f in range(HALVES)]
+            banks = [psum.tile([P, BANK], F32, name="h_b%d_%d" % (s, f), tag="p%d" % (2 * (s % 2) + f)) for f in range(HALVES)]
             for a in range(KP):
                 c = slice(a * P, (a + 1) * P)
                 for f in range(HALVES):
                     j = slice(f * BANK, (f + 1) * BANK)
                     nc.tensor.matmul_mx(
                         out=banks[f][:], lhsT=w1_q[s][:, c].bitcast(FP8X4), lhsT_scale=w1_s[s][:, c],
-                        rhs=v_w[(a, f)].bitcast(FP8X4), rhs_scale=v_s[4 * a :, j], start=(a == 0), stop=(a == KP - 1),
+                        rhs=v_w[a][:, j].bitcast(FP8X4), rhs_scale=v_s[4 * a :, j], start=(a == 0), stop=(a == KP - 1),
                     )
             h_banks[s] = banks
 
         def copy_h(s):
-            t = ring.tile([P, S], F32, name="h%d" % s, tag="h", bufs=3)
+            t = ring.tile([P, S], F32, name="h%d" % s, tag="h", bufs=4)
             for f in range(HALVES):
                 j = slice(f * BANK, (f + 1) * BANK)
-                if (s, f) == (0, 0):
+                if s == 0:
                     nc.vector.tensor_copy(t[:, j], h_banks[s][f][:])
                 else:
                     nc.scalar.copy(t[:, j], h_banks[s][f][:])
             h_t[s] = t
 
         def look(s):
-            t = ring.tile([P, NP], F32, name="look%d" % s, tag="look%d" % (s % 2), align_bytes=64)
+            t = ring.tile([P, NP], F32, name="look%d" % s, tag="look", bufs=2)
             nc.scalar.activation(out=t[:], in_=h_t[s][:].indirect(pos1_t[:]), func=ACT.Sigmoid, bias=cols[:, s : s + 1])
             look_t[s] = t
 
@@ -221,7 +205,7 @@ def tile_list_weft_fault_repair_kernel(tc, tab_words, tab_scales, offs, pos1, po
             page_t[s] = t
 
         def weigh(s):
-            t = ring.tile([P, NP], F32, name="ww%d" % s, tag="ww", bufs=1)
+            t = ring.tile([P, NP], F32, name="ww%d" % s, tag="ww", bufs=2)
             nc.vector.tensor_tensor(t[:], weft_t[s], wgs_t[:], MULT)
             ww_t[s] = t
 
@@ -230,7 +214,7 @@ def tile_list_weft_fault_repair_kernel(tc, tab_words, tab_scales, offs, pos1, po
 
         def turn(s, src, first):
             if first:
-                sum_banks[s] = [psum.tile([P, PACK, P], F32, name="t_b%d_%d" % (s, f), tag=("o%d" if s == SLICES - 1 else "t%d") % f) for f in range(HALVES)]
+                sum_banks[s] = [psum.tile([P, PACK, P], F32, name="t_b%d_%d" % (s, f), tag="p%d" % (2 * (s % 2) + f)) for f in range(HALVES)]
             for f in range(HALVES):
                 for c in range(PACK):
                     jc = PACK * f + c
@@ -249,7 +233,7 @@ def tile_list_weft_fault_repair_kernel(tc, tab_words, tab_scales, offs, pos1, po
                 )
 
         def turn_back(b, q, tag):
-            zi = ring.tile([P, QUARTER * PACK], BF16, name="zi%d_%d" % (b, q), tag="zi", bufs=4, align_bytes=64)
+            zi = ring.tile([P, QUARTER * PACK], BF16, name="zi%d_%d" % (b, q), tag="zi%d" % q, align_bytes=64)
             bank = psum.tile([P, 2, 2, P], F32, name="w_b%d_%d" % (b, q), tag=tag)
             for c in range(2):
                 words = z_t[(b, q // 2)][:, 2 * (q % 2) + c, :].bitcast(F32)
@@ -283,7 +267,6 @@ def tile_list_weft_fault_repair_kernel(tc, tab_words, tab_scales, offs, pos1, po
 
         cast_w1(0)
         quant_w1(0)
-        gather_half(KP - 1, 1)
         first_product(0)
         copy_h(0)
         look(0)
@@ -293,37 +276,43 @@ def tile_list_weft_fault_repair_kernel(tc, tab_words, tab_scales, offs, pos1, po
         quant_w1(1)
         first_product(1)
         cast_w1(2)
-        turn(0, h_t[0], True)
+        quant_w1(2)
+        copy_h(1)
+        first_product(2)
         for s in range(SLICES):
             scatter(s)
-            turn(s, page_t[s], False)
             if s + 1 < SLICES:
-                copy_h(s + 1)
                 look(s + 1)
                 fill_page(s + 1)
                 weigh(s + 1)
+            if s >= 1:
+                round_z(s - 1)
+            if 1 <= s and s + 2 < SLICES:
+                first_product(s + 2)
             if s == 0:
                 cast_w1(3)
-            if s + 2 < SLICES:
-                quant_w1(s + 2)
-                first_product(s + 2)
+                quant_w1(3)
             if s + 4 < SLICES:
                 cast_w1(s + 4)
-            round_z(s)
-            if s + 1 < SLICES:
-                turn(s + 1, h_t[s + 1], True)
-            if s in (PACK, PACK + 1):
-                for g in range(2):
-                    turn_back(0, 2 * (s - PACK) + g, "w%d" % g)
-            if s == SLICES - 2:
-                for g in range(2):
-                    second_product(0, 0, g, "t%d" % g)
-        for q, tag in enumerate(("h0", "h1", "w0", "w1")):
-            turn_back(1, q, tag)
-        for q, tags in enumerate((None, "h%d", "o%d", "w%d")):
+                quant_w1(s + 4)
+            if s + 2 < SLICES:
+                copy_h(s + 2)
+            turn(s, h_t[s], True)
+            turn(s, page_t[s], False)
+            if s == PACK:
+                for q, tag in enumerate(("o0", "o1", "w0", "w1")):
+                    turn_back(0, q, tag)
+            if s == LAST - 1:
+                for q, tag in enumerate(("o%d", "w%d")):
+                    for g in range(2):
+                        second_product(0, q, g, tag % g)
+        round_z(LAST)
+        for q in range(4):
+            turn_back(1, q, "p%d" % q)
+        for q in range(4):
             for g in range(2):
-                if tags is not None:
-                    second_product(0, q, g, tags % g)
+                if q >= 2:
+                    second_product(0, q, g, "p%d" % (2 * (q - 2) + g))
             for g in range(2):
                 second_product(1, q, g)
                 store(q, g)

from contextlib import ExitStack

import concourse.mybir as mybir
from concourse.masks import make_identity

K, T, S, NP, H, N = 1536, 4096, 1024, 512, 1024, 512
FLOPS = 2 * K * H * S + 2 * H * N * S

F32 = mybir.dt.float32
BF16 = mybir.dt.bfloat16
I32 = mybir.dt.int32
U32 = mybir.dt.uint32
U16 = mybir.dt.uint16
U8 = mybir.dt.uint8
FP8X4 = mybir.dt.float8_e4m3fn_x4
FP4X4 = mybir.dt.float4_e2m1fn_x4
MULT = mybir.AluOpType.mult
ACT = mybir.ActivationFunctionType

P = 128
PACK = 4
K_PASS = P * PACK
BANK = 512
KP = K // K_PASS
HP = H // K_PASS
SLICES = H // P
HALVES = S // BANK
QUARTER = 2 * P
V_CASTS = [(1, 2), (2, 2), (3, 1), (3, 2)]
LAST = SLICES - 1


def tile_list_weft_fault_repair_kernel(tc, tab_words, tab_scales, offs, pos1, pos2, w1, thr, weft, skip, wgs, gain, w4_words, w4_scales, out):
    nc = tc.nc
    with ExitStack() as ctx:
        lists = ctx.enter_context(tc.tile_pool(name="lists", bufs=1))
        keep = ctx.enter_context(tc.tile_pool(name="keep", bufs=1))
        ring = ctx.enter_context(tc.tile_pool(name="ring", bufs=1))
        psum = ctx.enter_context(tc.psum_pool(name="psum", bufs=1))

        offs_t = lists.tile([P, S // 16], U16, name="offs_t")
        pos1_t = lists.tile([P, NP // 16], U16, name="pos1_t")
        pos2_t = lists.tile([P, NP // 16], U16, name="pos2_t")

        tab_s = ring.tile([P, T], U8, name="tab_s", tag="v_w1", align_bytes=64)
        rows = keep.tile([P, P], F32, name="rows")
        w4_s = keep.tile([P, HP, N], U8, name="w4_s", align_bytes=64)
        w4_w = keep.tile([P, HP, 2 * N], U8, name="w4_w", align_bytes=64)
        ident = keep.tile([P, P], F32, name="ident")
        make_identity(nc, ident[:])
        nc.vector.memset(tab_s[:].bitcast(I32), 0)
        nc.vector.memset(rows[:], 0.0)
        nc.vector.memset(w4_s[:].rearrange("p a n -> p (a n)").bitcast(I32), 0)

        nc.sync.dma_start(offs_t[:], offs)
        tab_w = []

        def load_table(a):
            t = ring.tile([P, T], I32, name="tab_w%d" % a, tag="tab%d" % a, align_bytes=64)
            nc.sync.dma_start(t[:], tab_words[a].rearrange("p t i -> p (t i)").bitcast(I32))
            tab_w.append(t)

        load_table(0)
        for q in range(4):
            nc.sync.dma_start(tab_s[32 * q : 32 * q + 4 * KP, :].bitcast(I32), tab_scales[:, 4 * q : 4 * q + 4, :].bitcast(I32))
        load_table(1)
        for i, vec in enumerate((thr, skip, gain)):
            nc.sync.dma_start(rows[SLICES * i : SLICES * (i + 1), :], vec.rearrange("(s p) -> s p", p=P))

        w1_raw = {}
        weft_t = {}
        wgs_t = keep.tile([P, NP], F32, name="wgs_t")

        def load_w1(first, count):
            for a in range(KP):
                if first == 6:
                    t = late[:, a]
                else:
                    t = keep.tile([P, PACK, count * P], F32, name="w1_%d_%d" % (first, a))
                nc.sync.dma_start(t[:], w1[a * K_PASS : (a + 1) * K_PASS, first * P : (first + count) * P].rearrange("(p j) c -> p j c", j=PACK))
                for s in range(first, first + count):
                    w1_raw[(s, a)] = t[:, :, (s - first) * P : (s - first + 1) * P]

        def load_weft(first, count):
            t = keep.tile([P, count, NP], F32, name="weft_%d" % first)
            nc.sync.dma_start(t[:], weft[first * P : (first + count) * P, :].rearrange("(s p) m -> p s m", p=P))
            for s in range(first, first + count):
                weft_t[s] = t[:, s - first, :]

        load_table(KP - 1)
        load_w1(0, 1)
        nc.sync.dma_start(pos1_t[:], pos1)
        nc.sync.dma_start(pos2_t[:], pos2)
        load_w1(1, 1)
        nc.sync.dma_start(wgs_t[:], wgs)
        load_weft(0, 1)

        v_s = keep.tile([P, S], U8, name="v_s", align_bytes=64)
        v_w = {}

        for a in range(KP):
            t = ring.tile([P, S], U32, name="v_w%d" % a, tag=("v_w0", "v_w1", "tab1")[a], align_bytes=64)
            nc.vector.tensor_copy(t[:], tab_w[a][:].bitcast(U32).indirect(offs_t[:]))
            v_w[a] = t
            if a == 0:
                nc.vector.tensor_copy(v_s[:], tab_s[:].indirect(offs_t[:]))

        load_w1(2, 2)
        load_weft(1, 1)
        load_w1(4, 2)
        load_weft(2, 2)
        late = ring.tile([P, KP, PACK, 2 * P], F32, name="w1_late", tag="tab0", align_bytes=64)
        load_w1(6, 2)
        load_weft(4, 4)
        nc.sync.dma_start(w4_w[:].bitcast(I32), w4_words.rearrange("a p n -> p a n").bitcast(I32))

        for q in range(4):
            nc.sync.dma_start(
                w4_s[32 * q : 32 * q + 4, :, :].bitcast(I32),
                w4_scales[:, 4 * q : 4 * q + 4, :].rearrange("a r n -> r a n").bitcast(I32),
            )

        cols = keep.tile([P, 3 * SLICES], F32, name="cols")
        bank = psum.tile([P, BANK], F32, name="bank_c", tag="w1")
        nc.tensor.transpose(bank[:, 0:P], rows[:], ident[:])
        nc.scalar.copy(cols[:], bank[:, 0 : 3 * SLICES])
        gain_bc = keep.tile([P, SLICES, P], F32, name="gain_bc")
        for g in range(HP):
            bank = psum.tile([P, PACK, P], F32, name="bank_g%d" % g, tag="o%d" % g)
            for i in range(PACK):
                c = 2 * SLICES + PACK * g + i
                nc.tensor.transpose(bank[:, i, :], cols[:, c : c + 1].to_broadcast([P, P]), ident[:])
            nc.scalar.copy(
                gain_bc[:, PACK * g : PACK * (g + 1), :].rearrange("j i (u q e) -> j i u q e", u=2, e=2),
                bank[:].rearrange("j i (q u e) -> j i u q e", u=2, e=2),
            )

        w1_q = {}
        w1_s = [keep.tile([P, KP * P], U8, name="w1_s%d" % s, align_bytes=64) for s in range(SLICES)]
        w1_b = {}
        h_banks = {}
        h_t = {}
        look_t = {}
        page_t = {}
        ww_t = {}
        sum_banks = {}
        z_t = {(b, f): keep.tile([P, PACK, K_PASS], BF16, name="z_t%d_%d" % (b, f), align_bytes=64) for b in range(HP) for f in range(HALVES)}
        z_q = [keep.tile([P, S], U32, name="z_q%d" % b, align_bytes=64) for b in range(HP)]
        z_s = [keep.tile([P, S], U8, name="z_s%d" % b, align_bytes=64) for b in range(HP)]

        def cast_w1(s):
            t = ring.tile([P, KP, P * PACK], BF16, name="w1_b%d" % s, tag="w1_b", bufs=3, align_bytes=64)
            for a in range(KP):
                dst = t[:, a, :].rearrange("p (c i j) -> p c j i", i=4, j=PACK)
                src = w1_raw[(s, a)].rearrange("p j (c i) -> p c j i", i=4)
                if (s, a) in V_CASTS:
                    nc.vector.tensor_copy(dst, src)
                else:
                    nc.scalar.copy(dst, src)
            w1_b[s] = t

        def quant_w1(s):
            w1_q[s] = ring.tile([P, KP * P], U32, name="w1_q%d" % s, tag="tab2" if s == 0 else "w1_q%d" % s, align_bytes=64)
            if s == 0:
                for a in range(KP):
                    c = slice(a * P, (a + 1) * P)
                    nc.vector.quantize_mx(out=w1_q[s][:, c].bitcast(FP8X4), scales=w1_s[s][:, c], in_=w1_b[s][:, a, :])
            else:
                nc.vector.quantize_mx(out=w1_q[s][:].bitcast(FP8X4), scales=w1_s[s][:], in_=w1_b[s][:].rearrange("p a c -> p (a c)"))

        def first_product(s):
            banks = [psum.tile([P, BANK], F32, name="h_b%d_%d" % (s, f), tag="p%d" % (2 * (s % 2) + f)) for f in range(HALVES)]
            for a in range(KP):
                c = slice(a * P, (a + 1) * P)
                for f in range(HALVES):
                    j = slice(f * BANK, (f + 1) * BANK)
                    nc.tensor.matmul_mx(
                        out=banks[f][:], lhsT=w1_q[s][:, c].bitcast(FP8X4), lhsT_scale=w1_s[s][:, c],
                        rhs=v_w[a][:, j].bitcast(FP8X4), rhs_scale=v_s[4 * a :, j], start=(a == 0), stop=(a == KP - 1),
                    )
            h_banks[s] = banks

        def copy_h(s):
            t = ring.tile([P, S], F32, name="h%d" % s, tag="h", bufs=4)
            for f in range(HALVES):
                j = slice(f * BANK, (f + 1) * BANK)
                if s == 0:
                    nc.vector.tensor_copy(t[:, j], h_banks[s][f][:])
                else:
                    nc.scalar.copy(t[:, j], h_banks[s][f][:])
            h_t[s] = t

        def look(s):
            t = ring.tile([P, NP], F32, name="look%d" % s, tag="look", bufs=2)
            nc.scalar.activation(out=t[:], in_=h_t[s][:].indirect(pos1_t[:]), func=ACT.Sigmoid, bias=cols[:, s : s + 1])
            look_t[s] = t

        def fill_page(s):
            t = ring.tile([P, S], F32, name="page%d" % s, tag="page", bufs=3)
            col = cols[:, SLICES + s : SLICES + s + 1]
            if s == 0:
                nc.vector.tensor_scalar(out=t[:], in0=h_t[s][:], scalar1=col, scalar2=None, op0=MULT)
            else:
                nc.scalar.activation(out=t[:], in_=h_t[s][:], func=ACT.Copy, scale=col)
            page_t[s] = t

        def weigh(s):
            t = ring.tile([P, NP], F32, name="ww%d" % s, tag="ww", bufs=2)
            nc.vector.tensor_tensor(t[:], weft_t[s], wgs_t[:], MULT)
            ww_t[s] = t

        def scatter(s):
            nc.vector.tensor_tensor(page_t[s][:].indirect(pos2_t[:]), look_t[s][:], ww_t[s][:], MULT)

        def turn(s, src, first):
            if first:
                sum_banks[s] = [psum.tile([P, PACK, P], F32, name="t_b%d_%d" % (s, f), tag="p%d" % (2 * (s % 2) + f)) for f in range(HALVES)]
            for f in range(HALVES):
                for c in range(PACK):
                    jc = PACK * f + c
                    nc.tensor.matmul(
                        sum_banks[s][f][:, c, :], src[:, jc * P : (jc + 1) * P], ident[:], is_transpose=True,
                        start=(first and c == 0), stop=(not first and c == PACK - 1),
                    )

        def round_z(s):
            b, i = divmod(s, PACK)
            for f in range(HALVES):
                nc.vector.tensor_tensor(
                    z_t[(b, f)][:].rearrange("j c (u i q e) -> j i u c q e", u=2, i=PACK, e=2)[:, i],
                    sum_banks[s][f][:].rearrange("j c (q u e) -> j u c q e", u=2, e=2),
                    gain_bc[:, s : s + 1, :].to_broadcast([P, PACK, P]).rearrange("j c (u q e) -> j u c q e", u=2, e=2), MULT,
                )

        def turn_back(b, q, tag):
            zi = ring.tile([P, QUARTER * PACK], BF16, name="zi%d_%d" % (b, q), tag="zi%d" % q, align_bytes=64)
            bank = psum.tile([P, 2, 2, P], F32, name="w_b%d_%d" % (b, q), tag=tag)
            for c in range(2):
                words = z_t[(b, q // 2)][:, 2 * (q % 2) + c, :].bitcast(F32)
                for u in range(2):
                    nc.tensor.transpose(bank[:, c, u, :], words[:, u * P : (u + 1) * P], ident[:])
            nc.scalar.copy(zi[:].bitcast(F32).rearrange("p (c j u) -> p c j u", c=2, u=2), bank[:].rearrange("p c u j -> p c j u"))
            j = slice(q * QUARTER, (q + 1) * QUARTER)
            nc.vector.quantize_mx(out=z_q[b][:, j].bitcast(FP8X4), scales=z_s[b][:, j], in_=zi[:])

        out_banks = {}

        def second_product(b, q, g, tag=None):
            if b == 0:
                out_banks[(q, g)] = psum.tile([P, 2, QUARTER], F32, name="o_b%d_%d" % (q, g), tag=tag)
            j = slice(q * QUARTER, (q + 1) * QUARTER)
            for m in range(2):
                n = 2 * g + m
                nc.tensor.matmul_mx(
                    out=out_banks[(q, g)][:, m, :], lhsT=w4_w[:, b, 2 * P * n : 2 * P * (n + 1)].bitcast(FP4X4), lhsT_scale=w4_s[:, b, P * n : P * (n + 1)],
                    rhs=z_q[b][:, j].bitcast(FP8X4), rhs_scale=z_s[b][:, j], start=(b == 0 and m == 0), stop=(b == HP - 1 and m == 1),
                )

        def store(q, g):
            t = ring.tile([P, 2, QUARTER], F32, name="res%d_%d" % (q, g), tag="res", bufs=8)
            if g == 0:
                nc.scalar.copy(t[:], out_banks[(q, g)][:])
            else:
                nc.vector.tensor_copy(t[:], out_banks[(q, g)][:])
            rows_out = out[2 * g * P : 2 * (g + 1) * P, q * QUARTER : (q + 1) * QUARTER]
            nc.sync.dma_start(rows_out.rearrange("(m p) j -> p m j", p=P), t[:])

        cast_w1(0)
        quant_w1(0)
        first_product(0)
        copy_h(0)
        look(0)
        fill_page(0)
        weigh(0)
        cast_w1(1)
        quant_w1(1)
        first_product(1)
        cast_w1(2)
        quant_w1(2)
        copy_h(1)
        first_product(2)
        for s in range(SLICES):
            scatter(s)
            if s + 1 < SLICES:
                look(s + 1)
                fill_page(s + 1)
                weigh(s + 1)
            if s >= 1:
                round_z(s - 1)
            if 1 <= s and s + 2 < SLICES:
                first_product(s + 2)
            if s == 0:
                cast_w1(3)
                quant_w1(3)
            if s + 4 < SLICES:
                cast_w1(s + 4)
                quant_w1(s + 4)
            if s + 2 < SLICES:
                copy_h(s + 2)
            turn(s, h_t[s], True)
            turn(s, page_t[s], False)
            if s == PACK:
                for q, tag in enumerate(("o0", "o1", "w0", "w1")):
                    turn_back(0, q, tag)
            if s == LAST - 1:
                for q, tag in enumerate(("o%d", "w%d")):
                    for g in range(2):
                        second_product(0, q, g, tag % g)
        round_z(LAST)
        for q in range(4):
            turn_back(1, q, "p%d" % q)
        for q in range(4):
            for g in range(2):
                if q >= 2:
                    second_product(0, q, g, "p%d" % (2 * (q - 2) + g))
            for g in range(2):
                second_product(1, q, g)
                store(q, g)
